import numpy as np, ml_dtypes
CORES = [1,5,17,21,33,37,49,53]
N = 8
import mx_ref
BF = ml_dtypes.bfloat16
def entries(a):
    return np.ascontiguousarray(a.T).reshape(-1)
def table(e):
    return np.ascontiguousarray(np.reshape(e, (-1, 16)).T).astype(np.int32)
def cols(t, e):
    v = np.concatenate([t.reshape(128, -1, 4), np.zeros((128, 1, 4), BF)], axis=1)
    return np.ascontiguousarray(v[:, e]).reshape(128, -1)
def f(rng, *shape):
    return mx_ref.flush((rng.standard_normal(shape, dtype=np.float32) * np.exp2(rng.integers(-2, 3, shape[:-1] + (1,)))).astype(BF))
def wide(rng, *shape, cols=0):
    v = rng.standard_normal(shape, dtype=np.float32) * np.exp2(rng.integers(-12, 13, shape)).astype(np.float32)
    if cols: v *= np.repeat(np.exp2(rng.integers(-cols, cols + 1, shape[:-2] + (1, shape[-1] // 4))) * (rng.random(shape[:-2] + (1, shape[-1] // 4)) > 0.0625), 4, axis=-1).astype(np.float32)
    return mx_ref.flush(v.astype(BF))
B, K, O = 320, 96, 3
def order(r):
    return [(r + 1 + i) % N for i in range(N)]
def some(rng, where, n):
    e = np.full(K, -1); e[rng.permutation(K)[:n]] = rng.permutation(where)[:n]
    return table(e)
def setup_inputs(rng):
    return {"b": f(rng, N, 128, 4 * B), "x": f(rng, N, 128, 4 * K), "w": f(rng, N, 128, 512 * O), "pl": np.stack([some(rng, np.arange(B), int(rng.integers(K >> 1, K + 1))) for r in range(N)])}
def setup_inputs_same(rng):
    d = setup_inputs(rng)
    for i in range(50):
        at = rng.permutation(B)[:K]; quiet = rng.permutation(N)[:int(rng.integers(1, 3))].tolist()
        pl = [some(rng, at, 0 if r in quiet else int(rng.integers(K >> 2, (3 * K >> 2) + 1))) for r in range(N)]
        s = [set(entries(pl[r]).tolist()) - {-1} for r in range(N) if r not in quiet]
        if all(s[j] & s[k] for j in range(len(s)) for k in range(j)):
            d["pl"] = np.stack(pl); return d
    raise RuntimeError("no draw in which any two of the writing ranks have a place in common")
def setup_inputs_apart(rng):
    d = setup_inputs(rng); at, start = rng.permutation(B), int(rng.integers(N))
    pl = [None] * N
    for i in range(N):
        e = at[K * i:K * i + K]
        pl[(start + i) % N] = some(rng, e, len(e))
    d["pl"] = np.stack(pl); return d
def setup_inputs_runs(rng):
    d = setup_inputs(rng); p = rng.permutation(N)
    pl = [None] * N
    for i in range(N):
        if i == 0: at = np.arange(0)
        elif i % 3 == 1: at = (int(rng.integers(B)) + np.arange(K)) % B
        elif i % 3 == 2: at = np.flatnonzero(np.isin(np.arange(B) % 8, rng.permutation(8)[:8 * K // B]))
        else: at = rng.permutation(B)[:K - int(rng.integers(K >> 2, (3 * K >> 2) + 1))]
        at = rng.permutation(at); a = int(rng.integers(len(at) + 1))
        pl[p[i]] = table(np.concatenate([at[:a], np.full(K - len(at), -1), at[a:]]))
    d["pl"] = np.stack(pl); return d
def setup_inputs_halves(rng):
    d = setup_inputs(rng); at, start = rng.permutation(B), int(rng.integers(N))
    pl = [None] * N
    for i in range(N): pl[(start + i) % N] = some(rng, at[:B >> 1] if i < N >> 1 else at[B >> 1:], K)
    d["pl"] = np.stack(pl); return d
def setup_inputs_spread(rng):
    d = setup_inputs(rng); d["b"] = wide(rng, N, 128, 4 * B, cols=6); d["x"] = wide(rng, N, 128, 4 * K, cols=6); return d
def check_inputs(d):
    bad = []
    for r in range(N):
        e = entries(d["pl"][r])
        if e.min() < -1 or e.max() >= B: bad.append("pl")
        e = e[e >= 0]
        if len(set(e.tolist())) != len(e): bad.append("pl names a place twice")
    return bad
def reference(b, x, w, pl):
    y = np.zeros((N, 128, O * B), np.float32)
    for r in range(N):
        m = np.array(b[r]).reshape(128, B, 4)
        for s in order(r):
            e = entries(pl[s]); k = np.flatnonzero(e >= 0)
            m[:, e[k]] = x[s].reshape(128, K, 4)[:, k]
        q = mx_ref.quantize(m.reshape(128, 4 * B))
        for o in range(O):
            y[r][:, B * o:B * o + B] = mx_ref.matmul(mx_ref.quantize(cols(w[r], np.arange(128 * o, 128 * o + 128))), q)
    return {"y": y}

@@ -1,0 +1,269 @@
+from concourse.bass import DstId, RemoteDMATransfer
+from concourse.mybir import dt, AluOpType, ActivationFunctionType
+
+B, K, O = 320, 96, 3
+FAR, PASSED, MATE, OWN = B, B + 3 * K, B + 6 * K, B + 7 * K
+WIDE = B + 8 * K
+SLOT = 128
+HALF = B // 2
+PRIO = 2048
+
+SCRATCH = {
+    "lo": ("dram", [SLOT, 1], "int32"),
+    "land": ("dram", [8, SLOT, 1], "int32"),
+    "xt": ("sbuf", [128, 512], "bfloat16"),
+    "bt": ("sbuf", [128, 4 * B], "bfloat16"),
+    "wt": ("sbuf", [128, 512 * O], "bfloat16"),
+    "qc": ("sbuf", [128, WIDE + 32], "float8_e4m3fn_x4"),
+    "qs": ("sbuf", [128, WIDE + 32], "uint8"),
+    "wq": ("sbuf", [128, 128 * O], "float8_e4m3fn_x4"),
+    "ws": ("sbuf", [128, 128 * O], "uint8"),
+    "mq": ("sbuf", [128, B], "float8_e4m3fn_x4"),
+    "ms": ("sbuf", [128, B], "uint8"),
+    "idx": ("sbuf", [128, K], "int32"),
+    "six": ("sbuf", [128, K], "int32"),
+    "k16": ("sbuf", [128, K], "float32"),
+    "k95": ("sbuf", [128, K], "float32"),
+    "kk": ("sbuf", [128, K], "float32"),
+    "val": ("sbuf", [128, 4 * K], "float32"),
+    "part": ("sbuf", [128, 1], "int32"),
+    "par": ("sbuf", [128, 1], "int32"),
+    "pcol": ("sbuf", [128, 4], "float32"),
+    "di": ("sbuf", [128, 64], "int32"),
+    "dm": ("sbuf", [128, 64], "int32"),
+    "dump": ("sbuf", [128, 64], "float32"),
+    "pk": ("sbuf", [128, 64], "int32"),
+    "uneg": ("sbuf", [128, 64], "float32"),
+    "wneg": ("sbuf", [128, 64], "float32"),
+    "zl": ("sbuf", [128, 64], "float32"),
+    "tl": ("sbuf", [128, 64], "float32"),
+    "off": ("sbuf", [128, 32], "uint16"),
+    "win": ("sbuf", [128, B + SLOT], "float32"),
+    "dup": ("sbuf", [128, 20, 32], "float32"),
+    "tr": ("sbuf", [128, 20, 32], "float32"),
+    "best": ("sbuf", [128, 20], "int32"),
+    "bcol": ("sbuf", [128, 20], "int32"),
+    "pick": ("sbuf", [128, 20], "uint16"),
+    "yt": ("sbuf", [128, O * B], "float32"),
+    "ps": ("psum", [128, 512 * 6], "float32"),
+}
+SEMAPHORES = ["lp", "ow", "sx", "sb", "sw", "gi", "v", "mz", "qx", "qb", "qw", "loc", "al", "ac", "asc", "pc", "psc", "fc",
+              "fs", "ls", "lc", "sc", "sd", "of", "pa", "pb", "sa", "sb2", "m0", "m1", "m2", "m3", "m4", "m5",
+              "y0", "y1", "y2", "st"]
+
+
+def rank_program(g, core, T, topo):
+    rank = T.rank_of(core)
+    if rank is None:
+        return
+    cores, S = T.cores, T.sem
+    n = len(cores)
+    ADD, MUL, MIN, MAX, SUB = AluOpType.add, AluOpType.mult, AluOpType.min, AluOpType.max, AluOpType.subtract
+    LT, AND = AluOpType.is_lt, AluOpType.bitwise_and
+    COPY = ActivationFunctionType.Copy
+
+    def order(r):
+        return [(r + 1 + i) % n for i in range(n)]
+
+    def same_chip(a, b):
+        return topo.chip(cores[a]) == topo.chip(cores[b])
+
+    def far(r):
+        return [s for s in order(r)[:-1] if not same_chip(r, s) and topo.die(cores[s]) == topo.die(cores[r])]
+
+    def partner(r):
+        return [s for s in order(r)[:-1] if same_chip(r, s)][0]
+
+    def dst(r):
+        rid, pid, _ = topo.addr(cores[r])
+        return DstId(rid=rid, pnc=pid)
+
+    mate = partner(rank)
+    faraway = far(rank)
+    base = {rank: OWN, mate: MATE}
+    for d, s in enumerate(faraway):
+        base[s] = FAR + K * d
+    for d, s in enumerate(far(mate)):
+        base[s] = PASSED + K * d
+
+    eoff = topo.engines(core, cores[faraway[0]])
+    eall = topo.engines(core, cores[mate])
+    eon = [e for e in eall if e not in eoff]
+    moff = topo.mask(core, cores[faraway[0]])
+    mon = sum(1 << e for e in eon)
+    mall = topo.mask(core, cores[mate])
+
+    sy = g.sync
+    sy.dma_start(T.lo[0:K, :], T.pl[:, :]).then_inc(S.lp, 16)
+    sy.dma_start(T.lo[K:SLOT, :], T.pl[0:16, 0:2]).then_inc(S.lp, 16)
+    g.scalar.dma_start(T.xt[:, 0:4 * K], T.x[:, :]).then_inc(S.sx, 16)
+    g.scalar.dma_start(T.bt[:, :], T.b[:, :]).then_inc(S.sb, 16)
+    sy.dma_start(T.wt[:, :], T.w[:, :]).then_inc(S.sw, 16)
+
+    g.iota(T.idx[:, :], [[32, 3], [1, 2], [2, 16]], 0, 0).then_inc(S.gi, 1)
+    g.iota(T.di[:, :], [[0, 2], [1, 32]], 0, 32).then_inc(S.gi, 1)
+    g.iota(T.part[:, :], [[1, 1]], 0, 1).then_inc(S.gi, 1)
+    g.iota(T.win[:, 0:B], [[1, B]], 0, 0, allow_small_or_imprecise_dtypes=True).then_inc(S.gi, 1)
+    others = [s for s in order(rank)[:-1] if s != mate]
+    g.wait_ge(S.lp, 32)
+
+    def slot_at(r):
+        return T.land[order(r).index(rank)]
+
+    loc = 0
+    g.remote_dma_fused([
+        RemoteDMATransfer(dst_ids=[dst(s) for s in others], dma_engine_mask=moff, remote_sem=S.al,
+                          srcs=[T.lo[:, :]], dsts=[slot_at(s) for s in others]),
+        RemoteDMATransfer(dst_ids=[dst(mate)], dma_engine_mask=mon, remote_sem=S.al,
+                          srcs=[T.lo[:, :]], dsts=[slot_at(mate)]),
+    ], local_sem=S.loc)
+    loc += len(eoff) + len(eon)
+    n_lists = len(others) * len(eoff) + len(eon)
+
+    def at(r):
+        return FAR + K * far(r).index(rank)
+
+    g.wait_ge(S.qx, 1)
+    for codes in (True, False):
+        def view(a, m):
+            return T.qc[:, a:a + m].bitcast(dt.uint8) if codes else T.qs[:, a:a + m]
+        g.remote_dma_fused([
+            RemoteDMATransfer(dst_ids=[dst(s) for s in faraway], dma_engine_mask=moff, remote_sem=S.ac if codes else S.asc,
+                              srcs=[view(OWN, K)], dsts=[view(at(s), K) for s in faraway]),
+            RemoteDMATransfer(dst_ids=[dst(mate)], dma_engine_mask=mon, remote_sem=S.pc if codes else S.psc,
+                              srcs=[view(OWN, K)], dsts=[view(MATE, K)]),
+        ], local_sem=S.loc)
+        loc += len(eoff) + len(eon)
+    n_far, n_mate = len(faraway) * len(eoff), len(eon)
+    rid, pid, _ = topo.addr(cores[mate])
+    g.wait_ge(S.ac, n_far)
+    g.remote_dma(T.qc[:, PASSED:PASSED + 3 * K].bitcast(dt.uint8), T.qc[:, FAR:FAR + 3 * K].bitcast(dt.uint8),
+                 S.fc, S.loc, pid, rid, mon)
+    g.wait_ge(S.asc, n_far)
+    g.remote_dma(T.qs[:, PASSED:PASSED + 3 * K], T.qs[:, FAR:FAR + 3 * K], S.fs, S.loc, pid, rid, mall)
+    loc += len(eon) + len(eall)
+    g.wait_ge(S.loc, loc)
+
+    sy.wait_ge(S.lp, 32)
+    sy.dma_start(T.land[n - 1], T.lo[:, :]).then_inc(S.ow, 16)
+    for q, sem, blocks in ((sy, S.ls, (0, 1)), (g.scalar, S.lc, (2, 3))):
+        q.wait_ge(S.mz, 1)
+        q.wait_ge(S.ow, 16)
+        q.wait_ge(S.al, n_lists)
+        for k in blocks:
+            for u in (0, 1):
+                q.dma_start(T.pk[32 * k:32 * k + 16, 32 * u:32 * u + 32], T.land[4 * u:4 * u + 4]).then_inc(sem, 16)
+
+    ve, cnt = g.vector, [0]
+
+    def did(ins):
+        ins.then_inc(S.v, 1)
+        cnt[0] += 1
+
+    def settle():
+        ve.wait_ge(S.v, cnt[0])
+
+    did(ve.memset(T.xt[:, 4 * K:512], 0.0))
+    ve.memset(T.pk[:, :], 0).then_inc(S.mz, 1)
+    ve.wait_ge(S.sx, 16)
+    settle()
+    ve.quantize_mx(T.qc[:, OWN:OWN + 128], T.qs[:, OWN:OWN + 128], T.xt[:, :]).then_inc(S.qx, 1)
+    ve.wait_ge(S.gi, 4)
+    did(ve.tensor_scalar(T.six[:, :], T.idx[:, :], 1.0 / 6.0, -2.5 / 6.0, MUL, ADD))
+    did(ve.tensor_scalar(T.k16[:, :], T.idx[:, :], 16.0, None, MUL))
+    did(ve.tensor_scalar(T.par[:, :], T.part[:, :], 16, None, AND))
+    did(ve.tensor_scalar(T.dm[:, :], T.di[:, :], 127, None, AND))
+    settle()
+    did(ve.tensor_scalar(T.k95[:, :], T.six[:, :], 95.0, None, MUL))
+    did(ve.tensor_scalar(T.dump[:, :], T.dm[:, :], float(B), None, ADD))
+    o = order(rank)
+    first = [[PRIO * (4 * u + t + 1) + base[o[4 * u + t]] for u in (0, 1)] for t in range(4)]
+    for t in range(4):
+        did(ve.tensor_scalar(T.pcol[:, t:t + 1], T.par[:, :], (first[t][1] - first[t][0]) / 16.0, float(first[t][0]), MUL, ADD))
+    settle()
+    did(ve.tensor_tensor(T.kk[:, :], T.k16[:, :], T.k95[:, :], SUB))
+    settle()
+    for t in range(4):
+        did(ve.tensor_scalar(T.val[:, K * t:K * t + K], T.kk[:, :], T.pcol[:, t:t + 1], None, ADD))
+    ve.wait_ge(S.sb, 16)
+    ve.quantize_mx(T.qc[:, 0:B], T.qs[:, 0:B], T.bt[:, :]).then_inc(S.qb, 1)
+    ve.wait_ge(S.sw, 16)
+    ve.quantize_mx(T.wq[:, :], T.ws[:, :], T.wt[:, :]).then_inc(S.qw, 1)
+    ve.wait_ge(S.mz, 1)
+    ve.wait_ge(S.ls, 64)
+    ve.wait_ge(S.lc, 64)
+    did(ve.tensor_scalar(T.uneg[:, :], T.pk[:, :], 0.0, 8192.0, LT, MUL))
+    settle()
+    did(ve.tensor_tensor(T.wneg[:, :], T.uneg[:, :], T.dump[:, :], MIN))
+    settle()
+    for X in (0, 1):
+        did(ve.tensor_tensor(T.zl[:, 32 * X:32 * X + 32], T.pk[:, X:64:2], T.wneg[:, X:64:2], MAX))
+    settle()
+    did(ve.transpose(T.tl[:, :], T.zl[:, :]))
+    settle()
+    for X in (0, 1):
+        did(ve.tensor_copy(T.off[:, X:32:2], T.tl[:, 32 * X:32 * X + 16]))
+    for t in range(4):
+        settle()
+        ins = ve.tensor_copy(T.win[:, :].indirect(T.off[:, 8 * t:8 * t + 6]), T.val[:, K * t:K * t + K])
+        if t < 3:
+            did(ins)
+        else:
+            ins.then_inc(S.sc, 1)
+    ve.wait_ge(S.sc, 1)
+    did(ve.tensor_copy(T.dup[:, :, 0:16], T.win[:, 0:B]))
+    settle()
+    ve.wait_ge(S.sd, 1)
+    did(ve.transpose(T.tr[:, :, :], T.dup[:, :, :]))
+    settle()
+    did(ve.tensor_tensor(T.best[:, :], T.tr[:, :, 0], T.tr[:, :, 16], MAX))
+    settle()
+    did(ve.tensor_scalar(T.bcol[:, :], T.best[:, :], PRIO - 1, None, AND))
+    settle()
+    ve.tensor_copy(T.pick[:, :], T.bcol[:, :]).then_inc(S.of, 1)
+    ve.wait_ge(S.of, 1)
+    ve.wait_ge(S.qx, 1)
+    ve.wait_ge(S.qb, 1)
+    ve.wait_ge(S.pc, n_mate)
+    ve.wait_ge(S.ac, n_far)
+    ve.wait_ge(S.fc, len(eon))
+    for h, sem in ((0, S.pa), (1, S.pb)):
+        ve.tensor_copy(T.mq[:, HALF * h:HALF * h + HALF].bitcast(dt.uint32),
+                       T.qc[:, 0:WIDE].bitcast(dt.uint32).indirect(T.pick[:, 10 * h:10 * h + 10])).then_inc(sem, 1)
+
+    sl = g.scalar
+    sl.wait_ge(S.sc, 1)
+    sl.activation(T.dup[:, :, 16:32], T.win[:, 0:B], COPY).then_inc(S.sd, 1)
+    sl.wait_ge(S.qx, 1)
+    sl.wait_ge(S.qb, 1)
+    sl.wait_ge(S.of, 1)
+    sl.wait_ge(S.psc, n_mate)
+    sl.wait_ge(S.asc, n_far)
+    sl.wait_ge(S.fs, len(eall))
+    for h, sem in ((0, S.sa), (1, S.sb2)):
+        sl.activation(T.ms[:, HALF * h:HALF * h + HALF], T.qs[:, 0:WIDE].indirect(T.pick[:, 10 * h:10 * h + 10]), COPY).then_inc(sem, 1)
+
+    te = g.tensor
+    runs = [(0, 0), (1, 0), (0, 1), (1, 1), (2, 0), (2, 1)]
+    te.wait_ge(S.qw, 1)
+    waited = []
+    for i, (r, h) in enumerate(runs):
+        if h not in waited:
+            te.wait_ge((S.pa, S.pb)[h], 1)
+            te.wait_ge((S.sa, S.sb2)[h], 1)
+            waited.append(h)
+        te.matmul_mx(T.ps[:, 512 * i:512 * i + HALF], T.wq[:, 128 * r:128 * r + 128], T.ws[:, 128 * r:128 * r + 128],
+                     T.mq[:, HALF * h:HALF * h + HALF], T.ms[:, HALF * h:HALF * h + HALF], True, True).then_inc(S["m%d" % i], 1)
+    for i, (r, h) in enumerate(runs):
+        out = T.yt[:, B * r + HALF * h:B * r + HALF * h + HALF]
+        src = T.ps[:, 512 * i:512 * i + HALF]
+        if (r, h) in ((0, 0), (0, 1), (2, 1)):
+            ve.wait_ge(S["m%d" % i], 1)
+            ve.tensor_copy(out, src).then_inc(S["y%d" % r], 1)
+        else:
+            sl.wait_ge(S["m%d" % i], 1)
+            sl.activation(out, src, COPY).then_inc(S["y%d" % r], 1)
+    for r in range(O):
+        sy.wait_ge(S["y%d" % r], 2)
+        sy.dma_start(T.y[:, B * r:B * r + B], T.yt[:, B * r:B * r + B]).then_inc(S.st, 16)
+    sy.wait_ge(S.st, 48)

@@ -8,47 +8,25 @@ SLOT = 128
 HALF = B // 2
 PRIO = 2048
 
+
+def _sb(n, t):
+    return ("sbuf", [128, n], t)
+
+
+F, I, U, H, C = "float32", "int32", "uint16", "bfloat16", "float8_e4m3fn_x4"
 SCRATCH = {
-    "lo": ("dram", [SLOT, 1], "int32"),
-    "land": ("dram", [8, SLOT, 1], "int32"),
-    "xt": ("sbuf", [128, 512], "bfloat16"),
-    "bt": ("sbuf", [128, 4 * B], "bfloat16"),
-    "wt": ("sbuf", [128, 512 * O], "bfloat16"),
-    "qc": ("sbuf", [128, WIDE + 32], "float8_e4m3fn_x4"),
-    "qs": ("sbuf", [128, WIDE + 32], "uint8"),
-    "wq": ("sbuf", [128, 128 * O], "float8_e4m3fn_x4"),
-    "ws": ("sbuf", [128, 128 * O], "uint8"),
-    "mq": ("sbuf", [128, B], "float8_e4m3fn_x4"),
-    "ms": ("sbuf", [128, B], "uint8"),
-    "idx": ("sbuf", [128, K], "int32"),
-    "six": ("sbuf", [128, K], "int32"),
-    "k16": ("sbuf", [128, K], "float32"),
-    "k95": ("sbuf", [128, K], "float32"),
-    "kk": ("sbuf", [128, K], "float32"),
-    "val": ("sbuf", [128, 4 * K], "float32"),
-    "part": ("sbuf", [128, 1], "int32"),
-    "par": ("sbuf", [128, 1], "int32"),
-    "pcol": ("sbuf", [128, 4], "float32"),
-    "di": ("sbuf", [128, 64], "int32"),
-    "dm": ("sbuf", [128, 64], "int32"),
-    "dump": ("sbuf", [128, 64], "float32"),
-    "pk": ("sbuf", [128, 64], "int32"),
-    "uneg": ("sbuf", [128, 64], "float32"),
-    "wneg": ("sbuf", [128, 64], "float32"),
-    "zl": ("sbuf", [128, 64], "float32"),
-    "tl": ("sbuf", [128, 64], "float32"),
-    "off": ("sbuf", [128, 32], "uint16"),
-    "win": ("sbuf", [128, B + SLOT], "float32"),
-    "dup": ("sbuf", [128, 20, 32], "float32"),
-    "tr": ("sbuf", [128, 20, 32], "float32"),
-    "best": ("sbuf", [128, 20], "int32"),
-    "bcol": ("sbuf", [128, 20], "int32"),
-    "pick": ("sbuf", [128, 20], "uint16"),
-    "yt": ("sbuf", [128, O * B], "float32"),
-    "ps": ("psum", [128, 512 * 6], "float32"),
+    "lo": ("dram", [SLOT, 1], I), "land": ("dram", [8, SLOT, 1], I),
+    "xt": _sb(512, H), "bt": _sb(4 * B, H), "wt": _sb(512 * O, H),
+    "qc": _sb(WIDE + 32, C), "qs": _sb(WIDE + 32, "uint8"), "wq": _sb(128 * O, C), "ws": _sb(128 * O, "uint8"),
+    "mq": _sb(B, C), "ms": _sb(B, "uint8"),
+    "idx": _sb(K, I), "six": _sb(K, I), "k16": _sb(K, F), "k95": _sb(K, F), "kk": _sb(K, F), "val": _sb(4 * K, F),
+    "part": _sb(1, I), "par": _sb(1, I), "pcol": _sb(4, F), "di": _sb(64, I), "dm": _sb(64, I), "dump": _sb(64, F),
+    "pk": _sb(64, I), "zl": _sb(64, F), "tl": _sb(64, F), "off": _sb(32, U), "bl": _sb(B, F),
+    "win": _sb(SLOT * (B + 1), F), "dup": ("sbuf", [128, 20, 32], F), "tr": ("sbuf", [128, 20, 32], F),
+    "best": _sb(20, I), "bcol": _sb(20, I), "pick": _sb(20, U), "yt": _sb(O * B, F), "ps": ("psum", [128, 512 * 6], F),
 }
-SEMAPHORES = ["lp", "ow", "sx", "sb", "sw", "gi", "v", "mz", "qx", "qb", "qw", "loc", "al", "ac", "asc", "pc", "psc", "fc",
-              "fs", "ls", "lc", "sc", "sd", "of", "pa", "pb", "sa", "sb2", "m0", "m1", "m2", "m3", "m4", "m5",
+SEMAPHORES = ["lp", "ow", "sx", "sb", "sw", "gi", "gb", "wi", "v", "mz", "qx", "qb", "qw", "loc", "al", "ac", "asc", "pc",
+              "psc", "fc", "fs", "ls", "lc", "sc", "sd", "of", "pa", "pb", "sa", "sb2", "m0", "m1", "m2", "m3", "m4", "m5",
               "y0", "y1", "y2", "st"]
 
 
@@ -58,8 +36,7 @@ def rank_program(g, core, T, topo):
         return
     cores, S = T.cores, T.sem
     n = len(cores)
-    ADD, MUL, MIN, MAX, SUB = AluOpType.add, AluOpType.mult, AluOpType.min, AluOpType.max, AluOpType.subtract
-    LT, AND = AluOpType.is_lt, AluOpType.bitwise_and
+    ADD, MUL, MAX, SUB, AND = AluOpType.add, AluOpType.mult, AluOpType.max, AluOpType.subtract, AluOpType.bitwise_and
     COPY = ActivationFunctionType.Copy
 
     def order(r):
@@ -93,32 +70,29 @@ def rank_program(g, core, T, topo):
     mon = sum(1 << e for e in eon)
     mall = topo.mask(core, cores[mate])
 
-    sy = g.sync
+    sy, sl = g.sync, g.scalar
     sy.dma_start(T.lo[0:K, :], T.pl[:, :]).then_inc(S.lp, 16)
     sy.dma_start(T.lo[K:SLOT, :], T.pl[0:16, 0:2]).then_inc(S.lp, 16)
-    g.scalar.dma_start(T.xt[:, 0:4 * K], T.x[:, :]).then_inc(S.sx, 16)
-    g.scalar.dma_start(T.bt[:, :], T.b[:, :]).then_inc(S.sb, 16)
+    sl.dma_start(T.xt[:, 0:4 * K], T.x[:, :]).then_inc(S.sx, 16)
+    sl.dma_start(T.bt[:, :], T.b[:, :]).then_inc(S.sb, 16)
     sy.dma_start(T.wt[:, :], T.w[:, :]).then_inc(S.sw, 16)
 
     g.iota(T.idx[:, :], [[32, 3], [1, 2], [2, 16]], 0, 0).then_inc(S.gi, 1)
     g.iota(T.di[:, :], [[0, 2], [1, 32]], 0, 32).then_inc(S.gi, 1)
     g.iota(T.part[:, :], [[1, 1]], 0, 1).then_inc(S.gi, 1)
-    g.iota(T.win[:, 0:B], [[1, B]], 0, 0, allow_small_or_imprecise_dtypes=True).then_inc(S.gi, 1)
     others = [s for s in order(rank)[:-1] if s != mate]
+    half = len(others) // 2
     g.wait_ge(S.lp, 32)
 
     def slot_at(r):
         return T.land[order(r).index(rank)]
 
-    loc = 0
     g.remote_dma_fused([
-        RemoteDMATransfer(dst_ids=[dst(s) for s in others], dma_engine_mask=moff, remote_sem=S.al,
-                          srcs=[T.lo[:, :]], dsts=[slot_at(s) for s in others]),
-        RemoteDMATransfer(dst_ids=[dst(mate)], dma_engine_mask=mon, remote_sem=S.al,
-                          srcs=[T.lo[:, :]], dsts=[slot_at(mate)]),
-    ], local_sem=S.loc)
-    loc += len(eoff) + len(eon)
-    n_lists = len(others) * len(eoff) + len(eon)
+        RemoteDMATransfer(dst_ids=[dst(s) for s in to], dma_engine_mask=1 << e, remote_sem=S.al,
+                          srcs=[T.lo[:, :]], dsts=[slot_at(s) for s in to])
+        for e, to in ((eoff[0], others[:half]), (eoff[len(eoff) // 2], others[half:] + [mate]))], local_sem=S.loc)
+    loc = 2
+    n_lists = n - 1
 
     def at(r):
         return FAR + K * far(r).index(rank)
@@ -135,6 +109,7 @@ def rank_program(g, core, T, topo):
         ], local_sem=S.loc)
         loc += len(eoff) + len(eon)
     n_far, n_mate = len(faraway) * len(eoff), len(eon)
+    g.iota(T.bl[:, :], [[1, B]], 0, 0, allow_small_or_imprecise_dtypes=True).then_inc(S.gb, 1)
     rid, pid, _ = topo.addr(cores[mate])
     g.wait_ge(S.ac, n_far)
     g.remote_dma(T.qc[:, PASSED:PASSED + 3 * K].bitcast(dt.uint8), T.qc[:, FAR:FAR + 3 * K].bitcast(dt.uint8),
@@ -144,9 +119,10 @@ def rank_program(g, core, T, topo):
     loc += len(eon) + len(eall)
     g.wait_ge(S.loc, loc)
 
+    places = T.win[:, SLOT:SLOT * (B + 1):SLOT]
     sy.wait_ge(S.lp, 32)
     sy.dma_start(T.land[n - 1], T.lo[:, :]).then_inc(S.ow, 16)
-    for q, sem, blocks in ((sy, S.ls, (0, 1)), (g.scalar, S.lc, (2, 3))):
+    for q, sem, blocks in ((sy, S.ls, (0, 1)), (sl, S.lc, (2, 3))):
         q.wait_ge(S.mz, 1)
         q.wait_ge(S.ow, 16)
         q.wait_ge(S.al, n_lists)
@@ -168,14 +144,14 @@ def rank_program(g, core, T, topo):
     ve.wait_ge(S.sx, 16)
     settle()
     ve.quantize_mx(T.qc[:, OWN:OWN + 128], T.qs[:, OWN:OWN + 128], T.xt[:, :]).then_inc(S.qx, 1)
-    ve.wait_ge(S.gi, 4)
+    ve.wait_ge(S.gi, 3)
     did(ve.tensor_scalar(T.six[:, :], T.idx[:, :], 1.0 / 6.0, -2.5 / 6.0, MUL, ADD))
     did(ve.tensor_scalar(T.k16[:, :], T.idx[:, :], 16.0, None, MUL))
     did(ve.tensor_scalar(T.par[:, :], T.part[:, :], 16, None, AND))
-    did(ve.tensor_scalar(T.dm[:, :], T.di[:, :], 127, None, AND))
+    did(ve.tensor_scalar(T.dm[:, :], T.di[:, :], SLOT - 1, None, AND))
     settle()
     did(ve.tensor_scalar(T.k95[:, :], T.six[:, :], 95.0, None, MUL))
-    did(ve.tensor_scalar(T.dump[:, :], T.dm[:, :], float(B), None, ADD))
+    did(ve.tensor_scalar(T.dump[:, :], T.dm[:, :], -1.0 / SLOT, -1.0 / SLOT, MUL, ADD))
     o = order(rank)
     first = [[PRIO * (4 * u + t + 1) + base[o[4 * u + t]] for u in (0, 1)] for t in range(4)]
     for t in range(4):
@@ -187,22 +163,22 @@ def rank_program(g, core, T, topo):
         did(ve.tensor_scalar(T.val[:, K * t:K * t + K], T.kk[:, :], T.pcol[:, t:t + 1], None, ADD))
     ve.wait_ge(S.sb, 16)
     ve.quantize_mx(T.qc[:, 0:B], T.qs[:, 0:B], T.bt[:, :]).then_inc(S.qb, 1)
+    ve.wait_ge(S.gb, 1)
+    ve.tensor_copy(places, T.bl[:, :]).then_inc(S.wi, 1)
     ve.wait_ge(S.sw, 16)
     ve.quantize_mx(T.wq[:, :], T.ws[:, :], T.wt[:, :]).then_inc(S.qw, 1)
     ve.wait_ge(S.mz, 1)
+    ve.wait_ge(S.wi, 1)
+    settle()
     ve.wait_ge(S.ls, 64)
     ve.wait_ge(S.lc, 64)
-    did(ve.tensor_scalar(T.uneg[:, :], T.pk[:, :], 0.0, 8192.0, LT, MUL))
-    settle()
-    did(ve.tensor_tensor(T.wneg[:, :], T.uneg[:, :], T.dump[:, :], MIN))
-    settle()
     for X in (0, 1):
-        did(ve.tensor_tensor(T.zl[:, 32 * X:32 * X + 32], T.pk[:, X:64:2], T.wneg[:, X:64:2], MAX))
+        did(ve.tensor_tensor(T.zl[:, 32 * X:32 * X + 32], T.pk[:, X:64:2], T.dump[:, X:64:2], MAX))
     settle()
     did(ve.transpose(T.tl[:, :], T.zl[:, :]))
     settle()
     for X in (0, 1):
-        did(ve.tensor_copy(T.off[:, X:32:2], T.tl[:, 32 * X:32 * X + 16]))
+        did(ve.tensor_scalar(T.off[:, X:32:2], T.tl[:, 32 * X:32 * X + 16], float(SLOT), float(SLOT), MUL, ADD))
     for t in range(4):
         settle()
         ins = ve.tensor_copy(T.win[:, :].indirect(T.off[:, 8 * t:8 * t + 6]), T.val[:, K * t:K * t + K])
@@ -211,7 +187,7 @@ def rank_program(g, core, T, topo):
         else:
             ins.then_inc(S.sc, 1)
     ve.wait_ge(S.sc, 1)
-    did(ve.tensor_copy(T.dup[:, :, 0:16], T.win[:, 0:B]))
+    did(ve.tensor_copy(T.dup[:, :, 0:16], places))
     settle()
     ve.wait_ge(S.sd, 1)
     did(ve.transpose(T.tr[:, :, :], T.dup[:, :, :]))
@@ -231,9 +207,8 @@ def rank_program(g, core, T, topo):
         ve.tensor_copy(T.mq[:, HALF * h:HALF * h + HALF].bitcast(dt.uint32),
                        T.qc[:, 0:WIDE].bitcast(dt.uint32).indirect(T.pick[:, 10 * h:10 * h + 10])).then_inc(sem, 1)
 
-    sl = g.scalar
     sl.wait_ge(S.sc, 1)
-    sl.activation(T.dup[:, :, 16:32], T.win[:, 0:B], COPY).then_inc(S.sd, 1)
+    sl.activation(T.dup[:, :, 16:32], places, COPY).then_inc(S.sd, 1)
     sl.wait_ge(S.qx, 1)
     sl.wait_ge(S.qb, 1)
     sl.wait_ge(S.of, 1)

from concourse.bass import DstId, RemoteDMATransfer
from concourse.mybir import dt, AluOpType, ActivationFunctionType

B, K, O = 320, 96, 3
FAR, PASSED, MATE, OWN = B, B + 3 * K, B + 6 * K, B + 7 * K
WIDE = B + 8 * K
SLOT = 128
HALF = B // 2
PRIO = 2048


def _sb(n, t):
    return ("sbuf", [128, n], t)


F, I, U, H, C = "float32", "int32", "uint16", "bfloat16", "float8_e4m3fn_x4"
SCRATCH = {
    "lo": ("dram", [SLOT, 1], I), "land": ("dram", [8, SLOT, 1], I),
    "xt": _sb(512, H), "bt": _sb(4 * B, H), "wt": _sb(512 * O, H),
    "qc": _sb(WIDE + 32, C), "qs": _sb(WIDE + 32, "uint8"), "wq": _sb(128 * O, C), "ws": _sb(128 * O, "uint8"),
    "mq": _sb(B, C), "ms": _sb(B, "uint8"),
    "idx": _sb(K, I), "six": _sb(K, I), "k16": _sb(K, F), "k95": _sb(K, F), "kk": _sb(K, F), "val": _sb(4 * K, F),
    "part": _sb(1, I), "par": _sb(1, I), "pcol": _sb(4, F), "di": _sb(64, I), "dm": _sb(64, I), "dump": _sb(64, F),
    "pk": _sb(64, I), "zl": _sb(64, F), "tl": _sb(64, F), "off": _sb(32, U), "bl": _sb(B, F),
    "win": _sb(SLOT * (B + 1), F), "dup": ("sbuf", [128, 20, 32], F), "tr": ("sbuf", [128, 20, 32], F),
    "best": _sb(20, I), "bcol": _sb(20, I), "pick": _sb(20, U), "yt": _sb(O * B, F), "ps": ("psum", [128, 512 * 6], F),
}
SEMAPHORES = ["lp", "ow", "sx", "sb", "sw", "gi", "gb", "wi", "v", "mz", "qx", "qb", "qw", "loc", "al", "ac", "asc", "pc",
              "psc", "fc", "fs", "ls", "lc", "sc", "sd", "of", "pa", "pb", "sa", "sb2", "m0", "m1", "m2", "m3", "m4", "m5",
              "y0", "y1", "y2", "st"]


def rank_program(g, core, T, topo):
    rank = T.rank_of(core)
    if rank is None:
        return
    cores, S = T.cores, T.sem
    n = len(cores)
    ADD, MUL, MAX, SUB, AND = AluOpType.add, AluOpType.mult, AluOpType.max, AluOpType.subtract, AluOpType.bitwise_and
    COPY = ActivationFunctionType.Copy

    def order(r):
        return [(r + 1 + i) % n for i in range(n)]

    def same_chip(a, b):
        return topo.chip(cores[a]) == topo.chip(cores[b])

    def far(r):
        return [s for s in order(r)[:-1] if not same_chip(r, s) and topo.die(cores[s]) == topo.die(cores[r])]

    def partner(r):
        return [s for s in order(r)[:-1] if same_chip(r, s)][0]

    def dst(r):
        rid, pid, _ = topo.addr(cores[r])
        return DstId(rid=rid, pnc=pid)

    mate = partner(rank)
    faraway = far(rank)
    base = {rank: OWN, mate: MATE}
    for d, s in enumerate(faraway):
        base[s] = FAR + K * d
    for d, s in enumerate(far(mate)):
        base[s] = PASSED + K * d

    eoff = topo.engines(core, cores[faraway[0]])
    eall = topo.engines(core, cores[mate])
    eon = [e for e in eall if e not in eoff]
    moff = topo.mask(core, cores[faraway[0]])
    mon = sum(1 << e for e in eon)
    mall = topo.mask(core, cores[mate])

    sy, sl = g.sync, g.scalar
    sy.dma_start(T.lo[0:K, :], T.pl[:, :]).then_inc(S.lp, 16)
    sy.dma_start(T.lo[K:SLOT, :], T.pl[0:16, 0:2]).then_inc(S.lp, 16)
    sl.dma_start(T.xt[:, 0:4 * K], T.x[:, :]).then_inc(S.sx, 16)
    sl.dma_start(T.bt[:, :], T.b[:, :]).then_inc(S.sb, 16)
    sy.dma_start(T.wt[:, :], T.w[:, :]).then_inc(S.sw, 16)

    g.iota(T.idx[:, :], [[32, 3], [1, 2], [2, 16]], 0, 0).then_inc(S.gi, 1)
    g.iota(T.di[:, :], [[0, 2], [1, 32]], 0, 32).then_inc(S.gi, 1)
    g.iota(T.part[:, :], [[1, 1]], 0, 1).then_inc(S.gi, 1)
    others = [s for s in order(rank)[:-1] if s != mate]
    half = len(others) // 2
    g.wait_ge(S.lp, 32)

    def slot_at(r):
        return T.land[order(r).index(rank)]

    g.remote_dma_fused([
        RemoteDMATransfer(dst_ids=[dst(s) for s in to], dma_engine_mask=1 << e, remote_sem=S.al,
                          srcs=[T.lo[:, :]], dsts=[slot_at(s) for s in to])
        for e, to in ((eoff[0], others[:half]), (eoff[len(eoff) // 2], others[half:] + [mate]))], local_sem=S.loc)
    loc = 2
    n_lists = n - 1

    def at(r):
        return FAR + K * far(r).index(rank)

    g.wait_ge(S.qx, 1)
    for codes in (True, False):
        def view(a, m):
            return T.qc[:, a:a + m].bitcast(dt.uint8) if codes else T.qs[:, a:a + m]
        g.remote_dma_fused([
            RemoteDMATransfer(dst_ids=[dst(s) for s in faraway], dma_engine_mask=moff, remote_sem=S.ac if codes else S.asc,
                              srcs=[view(OWN, K)], dsts=[view(at(s), K) for s in faraway]),
            RemoteDMATransfer(dst_ids=[dst(mate)], dma_engine_mask=mon, remote_sem=S.pc if codes else S.psc,
                              srcs=[view(OWN, K)], dsts=[view(MATE, K)]),
        ], local_sem=S.loc)
        loc += len(eoff) + len(eon)
    n_far, n_mate = len(faraway) * len(eoff), len(eon)
    g.iota(T.bl[:, :], [[1, B]], 0, 0, allow_small_or_imprecise_dtypes=True).then_inc(S.gb, 1)
    rid, pid, _ = topo.addr(cores[mate])
    g.wait_ge(S.ac, n_far)
    g.remote_dma(T.qc[:, PASSED:PASSED + 3 * K].bitcast(dt.uint8), T.qc[:, FAR:FAR + 3 * K].bitcast(dt.uint8),
                 S.fc, S.loc, pid, rid, mon)
    g.wait_ge(S.asc, n_far)
    g.remote_dma(T.qs[:, PASSED:PASSED + 3 * K], T.qs[:, FAR:FAR + 3 * K], S.fs, S.loc, pid, rid, mall)
    loc += len(eon) + len(eall)
    g.wait_ge(S.loc, loc)

    places = T.win[:, SLOT:SLOT * (B + 1):SLOT]
    sy.wait_ge(S.lp, 32)
    sy.dma_start(T.land[n - 1], T.lo[:, :]).then_inc(S.ow, 16)
    for q, sem, blocks in ((sy, S.ls, (0, 1)), (sl, S.lc, (2, 3))):
        q.wait_ge(S.mz, 1)
        q.wait_ge(S.ow, 16)
        q.wait_ge(S.al, n_lists)
        for k in blocks:
            for u in (0, 1):
                q.dma_start(T.pk[32 * k:32 * k + 16, 32 * u:32 * u + 32], T.land[4 * u:4 * u + 4]).then_inc(sem, 16)

    ve, cnt = g.vector, [0]

    def did(ins):
        ins.then_inc(S.v, 1)
        cnt[0] += 1

    def settle():
        ve.wait_ge(S.v, cnt[0])

    did(ve.memset(T.xt[:, 4 * K:512], 0.0))
    ve.memset(T.pk[:, :], 0).then_inc(S.mz, 1)
    ve.wait_ge(S.sx, 16)
    settle()
    ve.quantize_mx(T.qc[:, OWN:OWN + 128], T.qs[:, OWN:OWN + 128], T.xt[:, :]).then_inc(S.qx, 1)
    ve.wait_ge(S.gi, 3)
    did(ve.tensor_scalar(T.six[:, :], T.idx[:, :], 1.0 / 6.0, -2.5 / 6.0, MUL, ADD))
    did(ve.tensor_scalar(T.k16[:, :], T.idx[:, :], 16.0, None, MUL))
    did(ve.tensor_scalar(T.par[:, :], T.part[:, :], 16, None, AND))
    did(ve.tensor_scalar(T.dm[:, :], T.di[:, :], SLOT - 1, None, AND))
    settle()
    did(ve.tensor_scalar(T.k95[:, :], T.six[:, :], 95.0, None, MUL))
    did(ve.tensor_scalar(T.dump[:, :], T.dm[:, :], -1.0 / SLOT, -1.0 / SLOT, MUL, ADD))
    o = order(rank)
    first = [[PRIO * (4 * u + t + 1) + base[o[4 * u + t]] for u in (0, 1)] for t in range(4)]
    for t in range(4):
        did(ve.tensor_scalar(T.pcol[:, t:t + 1], T.par[:, :], (first[t][1] - first[t][0]) / 16.0, float(first[t][0]), MUL, ADD))
    settle()
    did(ve.tensor_tensor(T.kk[:, :], T.k16[:, :], T.k95[:, :], SUB))
    settle()
    for t in range(4):
        did(ve.tensor_scalar(T.val[:, K * t:K * t + K], T.kk[:, :], T.pcol[:, t:t + 1], None, ADD))
    ve.wait_ge(S.sb, 16)
    ve.quantize_mx(T.qc[:, 0:B], T.qs[:, 0:B], T.bt[:, :]).then_inc(S.qb, 1)
    ve.wait_ge(S.gb, 1)
    ve.tensor_copy(places, T.bl[:, :]).then_inc(S.wi, 1)
    ve.wait_ge(S.sw, 16)
    ve.quantize_mx(T.wq[:, :], T.ws[:, :], T.wt[:, :]).then_inc(S.qw, 1)
    ve.wait_ge(S.mz, 1)
    ve.wait_ge(S.wi, 1)
    settle()
    ve.wait_ge(S.ls, 64)
    ve.wait_ge(S.lc, 64)
    for X in (0, 1):
        did(ve.tensor_tensor(T.zl[:, 32 * X:32 * X + 32], T.pk[:, X:64:2], T.dump[:, X:64:2], MAX))
    settle()
    did(ve.transpose(T.tl[:, :], T.zl[:, :]))
    settle()
    for X in (0, 1):
        did(ve.tensor_scalar(T.off[:, X:32:2], T.tl[:, 32 * X:32 * X + 16], float(SLOT), float(SLOT), MUL, ADD))
    for t in range(4):
        settle()
        ins = ve.tensor_copy(T.win[:, :].indirect(T.off[:, 8 * t:8 * t + 6]), T.val[:, K * t:K * t + K])
        if t < 3:
            did(ins)
        else:
            ins.then_inc(S.sc, 1)
    ve.wait_ge(S.sc, 1)
    did(ve.tensor_copy(T.dup[:, :, 0:16], places))
    settle()
    ve.wait_ge(S.sd, 1)
    did(ve.transpose(T.tr[:, :, :], T.dup[:, :, :]))
    settle()
    did(ve.tensor_tensor(T.best[:, :], T.tr[:, :, 0], T.tr[:, :, 16], MAX))
    settle()
    did(ve.tensor_scalar(T.bcol[:, :], T.best[:, :], PRIO - 1, None, AND))
    settle()
    ve.tensor_copy(T.pick[:, :], T.bcol[:, :]).then_inc(S.of, 1)
    ve.wait_ge(S.of, 1)
    ve.wait_ge(S.qx, 1)
    ve.wait_ge(S.qb, 1)
    ve.wait_ge(S.pc, n_mate)
    ve.wait_ge(S.ac, n_far)
    ve.wait_ge(S.fc, len(eon))
    for h, sem in ((0, S.pa), (1, S.pb)):
        ve.tensor_copy(T.mq[:, HALF * h:HALF * h + HALF].bitcast(dt.uint32),
                       T.qc[:, 0:WIDE].bitcast(dt.uint32).indirect(T.pick[:, 10 * h:10 * h + 10])).then_inc(sem, 1)

    sl.wait_ge(S.sc, 1)
    sl.activation(T.dup[:, :, 16:32], places, COPY).then_inc(S.sd, 1)
    sl.wait_ge(S.qx, 1)
    sl.wait_ge(S.qb, 1)
    sl.wait_ge(S.of, 1)
    sl.wait_ge(S.psc, n_mate)
    sl.wait_ge(S.asc, n_far)
    sl.wait_ge(S.fs, len(eall))
    for h, sem in ((0, S.sa), (1, S.sb2)):
        sl.activation(T.ms[:, HALF * h:HALF * h + HALF], T.qs[:, 0:WIDE].indirect(T.pick[:, 10 * h:10 * h + 10]), COPY).then_inc(sem, 1)

    te = g.tensor
    runs = [(0, 0), (1, 0), (0, 1), (1, 1), (2, 0), (2, 1)]
    te.wait_ge(S.qw, 1)
    waited = []
    for i, (r, h) in enumerate(runs):
        if h not in waited:
            te.wait_ge((S.pa, S.pb)[h], 1)
            te.wait_ge((S.sa, S.sb2)[h], 1)
            waited.append(h)
        te.matmul_mx(T.ps[:, 512 * i:512 * i + HALF], T.wq[:, 128 * r:128 * r + 128], T.ws[:, 128 * r:128 * r + 128],
                     T.mq[:, HALF * h:HALF * h + HALF], T.ms[:, HALF * h:HALF * h + HALF], True, True).then_inc(S["m%d" % i], 1)
    for i, (r, h) in enumerate(runs):
        out = T.yt[:, B * r + HALF * h:B * r + HALF * h + HALF]
        src = T.ps[:, 512 * i:512 * i + HALF]
        if (r, h) in ((0, 0), (0, 1), (2, 1)):
            ve.wait_ge(S["m%d" % i], 1)
            ve.tensor_copy(out, src).then_inc(S["y%d" % r], 1)
        else:
            sl.wait_ge(S["m%d" % i], 1)
            sl.activation(out, src, COPY).then_inc(S["y%d" % r], 1)
    for r in range(O):
        sy.wait_ge(S["y%d" % r], 2)
        sy.dma_start(T.y[:, B * r:B * r + B], T.yt[:, B * r:B * r + B]).then_inc(S.st, 16)
    sy.wait_ge(S.st, 48)
